import numpy as np
import ml_dtypes


def mxq(x, axis, fmt="e4m3"):
    dtype, down = {"e4m3": (ml_dtypes.float8_e4m3fn, 7), "e5m2": (ml_dtypes.float8_e5m2, 14)}[fmt]
    v = np.moveaxis(np.asarray(x, np.float32).astype(ml_dtypes.bfloat16).astype(np.float64), axis, -1)
    blocks = v.reshape(v.shape[:-1] + (-1, 32))
    amax = np.abs(blocks).max(-1, keepdims=True)
    byte = np.maximum(np.where(amax > 0, np.frexp(amax)[1] - 1 + 127, 0) - down, 1)
    scale = np.exp2(byte - 127.0)
    codes = (blocks / scale).astype(np.float32).astype(dtype).astype(np.float64)
    return np.moveaxis((codes * scale).reshape(v.shape), -1, axis)


WIDE = False


def mx_kscale(k):
    if not WIDE:
        return np.ones(k)
    levels = np.array([30, -30])
    if k % 512:
        return np.exp2(np.random.permutation(np.resize(levels, k // 32))).repeat(32)
    a = np.empty((k // 512, 16))
    for p in range(k // 512):
        a[p, :8] = np.random.permutation(np.resize(levels, 8))
        for g in range(8):
            far = levels[np.abs(levels - a[p, g]) >= 10]
            a[p, g + 8] = far[np.random.randint(len(far))]
    return np.exp2(a.ravel()).repeat(32)


def f64(x):
    return np.asarray(x).astype(np.float64)


def striped(idx):
    return np.tile(np.asarray(idx).reshape(-1, 16).T, (8, 1)).astype(np.uint16)


def unstriped(offs):
    return offs[:16].T.reshape(-1).astype(np.int64)


E2M1 = np.array([0.0, 0.5, 1.0, 1.5, 2.0, 3.0, 4.0, 6.0, -0.0, -0.5, -1.0, -1.5, -2.0, -3.0, -4.0, -6.0])


def pack_weight(w, fmt):
    k, n = w.shape
    w = f64(np.asarray(w, np.float32).astype(ml_dtypes.bfloat16)).reshape(k // 32, 32, n)
    amax = np.abs(w).max(1)
    if fmt in ("e4m3", "e5m2"):
        byte = np.frexp(amax)[1] - 1 + 127 - (7 if fmt == "e4m3" else 14)
    else:
        mant, ex = np.frexp(amax / 6.0)
        byte = np.where(mant > 0.5, ex, ex - 1) + 127
    byte = np.clip(np.where(amax > 0, byte, 1), 1, 254)
    scaled = (w * np.exp2(127.0 - byte)[:, None, :]).reshape(k, n).astype(np.float32)
    by_word = np.ascontiguousarray(scaled.reshape(k // 512, 128, 4, n).transpose(0, 1, 3, 2))
    if fmt in ("e4m3", "e5m2"):
        words = by_word.astype(ml_dtypes.float8_e4m3fn if fmt == "e4m3" else ml_dtypes.float8_e5m2).view(np.uint8)
    else:
        c = by_word.astype(ml_dtypes.float4_e2m1fn).view(np.uint8) & 0xF
        words = (c[..., 0::2] | (c[..., 1::2] << 4)).reshape(k // 512, 128, 2 * n)
    return np.ascontiguousarray(words), np.ascontiguousarray(byte.astype(np.uint8).reshape(k // 512, 16, n))


def unpack_weight(words, scales, fmt):
    g, _, n = scales.shape
    words = np.ascontiguousarray(words).reshape(g, 128, n, -1)
    if fmt in ("e4m3", "e5m2"):
        vals = words.view(ml_dtypes.float8_e4m3fn if fmt == "e4m3" else ml_dtypes.float8_e5m2).astype(np.float64)
    else:
        nib = np.empty((g, 128, n, 4), np.uint8)
        nib[..., 0::2] = words & 0xF
        nib[..., 1::2] = words >> 4
        vals = E2M1[nib]
    vals = vals * np.repeat(np.exp2(scales.astype(np.float64) - 127.0), 8, axis=1)[..., None]
    return vals.transpose(0, 1, 3, 2).reshape(g * 512, n)


def sigmoid(v):
    return 1.0 / (1.0 + np.exp(-v))


def sgn(shape):
    return np.random.uniform(0.5, 2.0, shape) * np.where(np.random.standard_normal(shape) < 0, -1.0, 1.0)


K, T, J, R, C, O, N, U = 512, 1024, 256, 512, 512, 256, 256, 128


def setup_inputs():
    n = np.random.standard_normal
    idx = np.random.permutation(T)[:J]
    idx2 = np.random.permutation(C)[:J]
    idx3 = np.random.permutation(C)[:C]
    idx4 = np.random.permutation(C)[:C]
    idx5 = np.random.permutation(C)[:O]
    idx6 = np.random.permutation(O)[:U]
    idx7 = np.random.permutation(O)[:U]
    fk = mx_kscale(K)
    fr = mx_kscale(R)
    xtp = pack_weight(n((K, T)) / fk[:, None], "e4m3")
    wp = pack_weight(n((K, R)) * 1 / np.sqrt(K) * fk[:, None], "e2m1")
    wbp = pack_weight(n((R, N)) * 1 / np.sqrt(R) / fr[:, None], "e5m2")
    return {
        "xt_words": xtp[0],
        "xt_scales": xtp[1],
        "w_words": wp[0],
        "w_scales": wp[1],
        "sa": (sgn((R, 1))).astype(np.float32),
        "sb": (np.random.uniform(0.5, 1.6, (R, 1)) * fr[:, None]).astype(np.float32),
        "sg": (sgn((R, 1))).astype(np.float32),
        "bg": (np.random.uniform(-2.0, 2.0, (R, 1))).astype(np.float32),
        "wb_words": wbp[0],
        "wb_scales": wbp[1],
        "so": (np.random.uniform(0.5, 1.6, (N, 1))).astype(np.float32),
        "sp": (np.random.uniform(0.5, 1.6, (N, 1))).astype(np.float32),
        "offs": striped(idx),
        "offs2": striped(idx2),
        "offs3": striped(idx3),
        "offs4": striped(idx4),
        "offs5": striped(idx5),
        "offs6": striped(idx6),
        "offs7": striped(idx7),
    }


def reference(xt_words, xt_scales, w_words, w_scales, sa, sb, sg, bg, wb_words, wb_scales, so, sp, offs, offs2, offs3, offs4, offs5, offs6, offs7):
    idx = unstriped(offs)
    idx2 = unstriped(offs2)
    idx3 = unstriped(offs3)
    idx4 = unstriped(offs4)
    idx5 = unstriped(offs5)
    idx6 = unstriped(offs6)
    idx7 = unstriped(offs7)
    xtu = unpack_weight(xt_words, xt_scales, "e4m3")
    wu = unpack_weight(w_words, w_scales, "e2m1")
    wbu = unpack_weight(wb_words, wb_scales, "e5m2")
    xtidxg = xtu[:, idx]
    a = wu.T @ xtidxg
    pw = np.zeros((R, C))
    pw[:, idx2] = a
    pg = np.maximum(pw, pw[:, idx3] * f64(sa) * sigmoid(pw[:, idx4] * f64(sg) + f64(bg)))
    hid = pg[:, idx5] * f64(sb)
    hidq = mxq(hid, 0, "e4m3")
    p = wbu.T @ hidq
    y = np.maximum(p[:, idx6] * f64(so), p[:, idx7] * f64(sp))
    return y

@@ -1,0 +1,212 @@
+from contextlib import ExitStack
+
+import concourse.mybir as mybir
+
+K, T, J, R, C, O, N, U = 512, 1024, 256, 512, 512, 256, 256, 128
+FLOPS = 2 * K * R * J + 2 * R * N * O
+
+F32 = mybir.dt.float32
+BF16 = mybir.dt.bfloat16
+I32 = mybir.dt.int32
+U32 = mybir.dt.uint32
+U16 = mybir.dt.uint16
+U8 = mybir.dt.uint8
+E4M3X4 = mybir.dt.float8_e4m3fn_x4
+E5M2X4 = mybir.dt.float8_e5m2_x4
+E2M1X4 = mybir.dt.float4_e2m1fn_x4
+ACT = mybir.ActivationFunctionType
+ALU = mybir.AluOpType
+
+P = 128
+PACK = 4
+QUADS = 4
+QUAD = 32
+BOARD = 2 * C
+
+
+def tile_list_gatedladder_solo_one_pairweighed_kernel(
+    tc, xt_words, xt_scales, w_words, w_scales, sa, sb, sg, bg, wb_words, wb_scales, so, sp,
+    offs, offs2, offs3, offs4, offs5, offs6, offs7, out,
+):
+    nc = tc.nc
+    with ExitStack() as ctx:
+        keep = ctx.enter_context(tc.tile_pool(name="keep", bufs=1))
+        psum = ctx.enter_context(tc.psum_pool(name="psum", bufs=1))
+
+        def list_tile(name, src):
+            return keep.tile(list(src.shape), U16, name=name)
+
+        l1, l2, l3, l4 = list_tile("l1", offs), list_tile("l2", offs2), list_tile("l3", offs3), list_tile("l4", offs4)
+        l5, l6, l7 = list_tile("l5", offs5), list_tile("l6", offs6), list_tile("l7", offs7)
+
+        xt_all = keep.tile([P, T], U32, align_bytes=64)
+        xs_all = keep.tile([P, T], U8, align_bytes=64, tag="xs_all_then_xt_pick")
+        xs_pick = keep.tile([P, J], U8, align_bytes=64)
+        w_raw = keep.tile([P, 2 * R], U8, align_bytes=64)
+        w_dealt = keep.tile([P, 2 * R], U8, align_bytes=64, tag="w_dealt_then_gate0")
+        ws_rows = keep.tile([PACK, QUADS, R // 4], I32, align_bytes=64)
+        ws_raw = keep.tile([P, R], U8, align_bytes=64)
+        ws_dealt = keep.tile([P, R], U8, align_bytes=64)
+        wb_sb = keep.tile([P, N], U32, align_bytes=64)
+        wbs_sb = keep.tile([P, N], U8, align_bytes=64)
+        sa_sb = keep.tile([P, PACK], F32)
+        sb_sb = keep.tile([P, PACK], F32)
+        sg_sb = keep.tile([P, PACK], F32)
+        bg_sb = keep.tile([P, PACK], F32)
+        so_sb = keep.tile([P, N // P], F32)
+        sp_sb = keep.tile([P, N // P], F32)
+        pw = [keep.tile([P, BOARD], F32, name="pw%d" % t) for t in range(PACK)]
+
+        nc.gpsimd.memset(xs_all[:].bitcast(I32), 0)
+        nc.vector.memset(ws_raw[:].bitcast(I32), 0)
+        nc.gpsimd.memset(wbs_sb[:].bitcast(I32), 0)
+        for t in range(PACK):
+            nc.vector.memset(pw[t][:, 0:C], 0.0)
+
+        def load_scale_rows(plane, rows):
+            for q in range(QUADS):
+                nc.sync.dma_start(
+                    plane[QUAD * q : QUAD * q + PACK, :].bitcast(I32),
+                    rows[0, PACK * q : PACK * (q + 1), :].bitcast(I32),
+                )
+
+        def load_by_row(dst, src):
+            nc.gpsimd.dma_start(dst[:], src.rearrange("(p t) o -> p (t o)", t=PACK))
+
+        nc.scalar.dma_start(xt_all[:].bitcast(I32), xt_words[0].rearrange("p n t -> p (n t)").bitcast(I32))
+        nc.sync.dma_start(ws_rows[:], w_scales[0].bitcast(I32).rearrange("(q r) c -> r q c", r=PACK))
+        nc.sync.dma_start(l1[:], offs)
+        nc.sync.dma_start(w_raw[:].bitcast(I32), w_words[0].bitcast(I32))
+        load_scale_rows(xs_all, xt_scales)
+        nc.sync.dma_start(l2[:], offs2)
+        load_by_row(sg_sb, sg)
+        load_by_row(bg_sb, bg)
+        nc.sync.dma_start(l4[:], offs4)
+        load_by_row(sa_sb, sa)
+        nc.sync.dma_start(l3[:], offs3)
+        load_by_row(sb_sb, sb)
+        nc.sync.dma_start(l5[:], offs5)
+        nc.sync.dma_start(wb_sb[:].bitcast(I32), wb_words[0].rearrange("p n t -> p (n t)").bitcast(I32))
+        load_scale_rows(wbs_sb, wb_scales)
+        with nc.allow_non_contiguous_dma(reason="one weight a partition"):
+            nc.sync.dma_start(so_sb[:], so.rearrange("(h p) o -> p (h o)", p=P))
+            nc.sync.dma_start(sp_sb[:], sp.rearrange("(h p) o -> p (h o)", p=P))
+        nc.sync.dma_start(l6[:], offs6)
+        nc.sync.dma_start(l7[:], offs7)
+
+        nc.scalar.copy(
+            w_dealt[:].bitcast(U16).rearrange("p (t m) -> p t m", t=PACK),
+            w_raw[:].bitcast(U16).rearrange("p (m t) -> p t m", t=PACK),
+        )
+        for q in range(QUADS):
+            nc.vector.tensor_copy(ws_raw[QUAD * q : QUAD * q + PACK, :].bitcast(I32), ws_rows[:, q, :])
+        ws_src = ws_raw[:].rearrange("p (m t) -> p t m", t=PACK)
+        ws_dst = ws_dealt[:].rearrange("p (t m) -> p t m", t=PACK)
+        nc.vector.tensor_copy(ws_dst[:, 0, :], ws_src[:, 0, :])
+        nc.vector.tensor_copy(xs_pick[:], xs_all[:].indirect(l1[:]))
+        xt_pick = keep.tile([P, J], U32, align_bytes=64, tag="xs_all_then_xt_pick")
+        half = J // 2
+        for s in range(2):
+            nc.vector.tensor_copy(
+                xt_pick[:, half * s : half * (s + 1)],
+                xt_all[:].indirect(l1[:, half // 16 * s : half // 16 * (s + 1)]),
+            )
+        nc.vector.tensor_copy(ws_dst[:, 1:PACK, :], ws_src[:, 1:PACK, :])
+
+        def first_product(bank, t, cols):
+            nc.tensor.matmul_mx(
+                bank,
+                lhsT=w_dealt[:, 2 * P * t : 2 * P * (t + 1)].bitcast(E2M1X4),
+                lhsT_scale=ws_dealt[:, P * t : P * (t + 1)],
+                rhs=xt_pick[:, cols].bitcast(E4M3X4),
+                rhs_scale=xs_pick[:, cols],
+                start=True,
+                stop=True,
+            )
+
+        a_sb = keep.tile([P, PACK, J], F32)
+        for s in range(2):
+            cols = slice(half * s, half * (s + 1))
+            bank = psum.tile([P, half], F32, name="a_half%d" % s)
+            first_product(bank[:], 0, cols)
+            nc.scalar.copy(a_sb[:, 0, cols], bank[:])
+        for ts in ((1,), (2, 3)):
+            bank = psum.tile([P, len(ts), J], F32, name="a_bank%d" % ts[0])
+            for i, t in enumerate(ts):
+                first_product(bank[:, i, :], t, slice(0, J))
+            nc.scalar.copy(a_sb[:, ts[0] : ts[-1] + 1, :], bank[:])
+        for s in range(2):
+            nc.vector.tensor_copy(
+                pw[0][:].indirect(l2[:, half // 16 * s : half // 16 * (s + 1)]),
+                a_sb[:, 0, half * s : half * (s + 1)],
+            )
+        for t in range(1, PACK):
+            nc.vector.tensor_copy(pw[t][:].indirect(l2[:]), a_sb[:, t, :])
+
+        gate = [keep.tile([P, C], F32, name="gate0", align_bytes=64, tag="w_dealt_then_gate0")]
+        gate.extend(keep.tile([P, C], F32, name="gate%d" % t) for t in range(1, PACK))
+        term = [keep.tile([P, C], F32, name="term%d" % t) for t in range(PACK)]
+        for t in range(PACK):
+            nc.scalar.activation(
+                gate[t][:], pw[t][:].indirect(l4[:]), ACT.Sigmoid,
+                bias=bg_sb[:, t : t + 1], scale=sg_sb[:, t : t + 1],
+            )
+            nc.scalar.activation(term[t][:], pw[t][:].indirect(l3[:]), ACT.Copy, scale=sa_sb[:, t : t + 1])
+
+        gated = [keep.tile([P, C], F32, name="gated%d" % t) for t in range(PACK)]
+        pg = [keep.tile([P, C], F32, name="pg%d" % t) for t in range(PACK)]
+        for t in range(PACK):
+            nc.vector.tensor_tensor(gated[t][:], term[t][:], gate[t][:], ALU.mult)
+            nc.vector.tensor_tensor(pg[t][:], gated[t][:], pw[t][:, 0:C], ALU.max)
+
+        hid = keep.tile([P, PACK, O], F32)
+        for t in range(PACK - 1):
+            nc.scalar.activation(hid[:, t, :], pg[t][:].indirect(l5[:]), ACT.Copy, scale=sb_sb[:, t : t + 1])
+        part = O // 2
+        t = PACK - 1
+        for s in range(2):
+            nc.scalar.activation(
+                hid[:, t, part * s : part * (s + 1)],
+                pg[t][:].indirect(l5[:, part // 16 * s : part // 16 * (s + 1)]),
+                ACT.Copy, scale=sb_sb[:, t : t + 1],
+            )
+
+        hid_bf = keep.tile([P, O, PACK], BF16, align_bytes=64)
+        hq = keep.tile([P, O], U32, align_bytes=64)
+        hs = keep.tile([P, O], U8, align_bytes=64)
+        nc.vector.tensor_copy(hid_bf[:, :, 0:2], hid[:, 0:2, :].rearrange("p t o -> p o t"))
+        for s in range(2):
+            cols = slice(part * s, part * (s + 1))
+            nc.vector.tensor_copy(hid_bf[:, cols, 2:4], hid[:, 2:4, cols].rearrange("p t o -> p o t"))
+        for s in range(2):
+            cols = slice(part * s, part * (s + 1))
+            nc.vector.quantize_mx(
+                hq[:, cols].bitcast(E4M3X4), hs[:, cols], hid_bf[:, cols, :].rearrange("p o t -> p (o t)")
+            )
+
+        p_sb = [keep.tile([P, O], F32, name="p_sb%d" % h) for h in range(N // P)]
+        for s in range(2):
+            cols = slice(part * s, part * (s + 1))
+            for h in range(N // P):
+                p_bank = psum.tile([P, part], F32, name="p_bank%d_%d" % (s, h))
+                nc.tensor.matmul_mx(
+                    p_bank[:],
+                    lhsT=wb_sb[:, P * h : P * (h + 1)].bitcast(E5M2X4),
+                    lhsT_scale=wbs_sb[:, P * h : P * (h + 1)],
+                    rhs=hq[:, cols].bitcast(E4M3X4),
+                    rhs_scale=hs[:, cols],
+                    start=True,
+                    stop=True,
+                )
+                if h == 0:
+                    nc.scalar.copy(p_sb[h][:, cols], p_bank[:])
+                else:
+                    nc.vector.tensor_copy(p_sb[h][:, cols], p_bank[:])
+        for h in range(N // P):
+            first = keep.tile([P, U], F32, name="first%d" % h)
+            second = keep.tile([P, U], F32, name="second%d" % h)
+            y = keep.tile([P, U], F32, name="y%d" % h)
+            nc.scalar.activation(first[:], p_sb[h][:].indirect(l6[:]), ACT.Copy, scale=so_sb[:, h : h + 1])
+            nc.scalar.activation(second[:], p_sb[h][:].indirect(l7[:]), ACT.Copy, scale=sp_sb[:, h : h + 1])
+            nc.vector.tensor_tensor(y[:], first[:], second[:], ALU.max)
+            nc.sync.dma_start(out[P * h : P * (h + 1), :], y[:])

@@ -60,6 +60,10 @@ def tile_list_gatedladder_solo_one_pairweighed_kernel(
         nc.gpsimd.memset(xs_all[:].bitcast(I32), 0)
         nc.vector.memset(ws_raw[:].bitcast(I32), 0)
         nc.gpsimd.memset(wbs_sb[:].bitcast(I32), 0)
+        warm_in = keep.tile([P, 1], F32)
+        warm_out = keep.tile([P, 1], F32)
+        nc.gpsimd.memset(warm_in[:], 0.0)
+        nc.scalar.activation(warm_out[:], warm_in[:], ACT.Sigmoid)
         for t in range(PACK):
             nc.vector.memset(pw[t][:, 0:C], 0.0)
 

@@ -40,7 +40,7 @@ def tile_list_gatedladder_solo_one_pairweighed_kernel(
         l5, l6, l7 = list_tile("l5", offs5), list_tile("l6", offs6), list_tile("l7", offs7)
 
         xt_all = keep.tile([P, T], U32, align_bytes=64)
-        xs_all = keep.tile([P, T], U8, align_bytes=64, tag="xs_all_then_xt_pick")
+        xs_all = keep.tile([P, T], U8, align_bytes=64)
         xs_pick = keep.tile([P, J], U8, align_bytes=64)
         w_raw = keep.tile([P, 2 * R], U8, align_bytes=64)
         w_dealt = keep.tile([P, 2 * R], U8, align_bytes=64, tag="w_dealt_then_gate0")
@@ -57,15 +57,15 @@ def tile_list_gatedladder_solo_one_pairweighed_kernel(
         sp_sb = keep.tile([P, N // P], F32)
         pw = [keep.tile([P, BOARD], F32, name="pw%d" % t) for t in range(PACK)]
 
-        nc.gpsimd.memset(xs_all[:].bitcast(I32), 0)
-        nc.vector.memset(ws_raw[:].bitcast(I32), 0)
-        nc.gpsimd.memset(wbs_sb[:].bitcast(I32), 0)
+        nc.vector.memset(xs_all[:].bitcast(I32), 0)
         warm_in = keep.tile([P, 1], F32)
         warm_out = keep.tile([P, 1], F32)
-        nc.gpsimd.memset(warm_in[:], 0.0)
+        nc.vector.memset(warm_in[:], 0.0)
         nc.scalar.activation(warm_out[:], warm_in[:], ACT.Sigmoid)
+        nc.vector.memset(ws_raw[:].bitcast(I32), 0)
         for t in range(PACK):
             nc.vector.memset(pw[t][:, 0:C], 0.0)
+        nc.vector.memset(wbs_sb[:].bitcast(I32), 0)
 
         def load_scale_rows(plane, rows):
             for q in range(QUADS):
@@ -75,18 +75,18 @@ def tile_list_gatedladder_solo_one_pairweighed_kernel(
                 )
 
         def load_by_row(dst, src):
-            nc.gpsimd.dma_start(dst[:], src.rearrange("(p t) o -> p (t o)", t=PACK))
+            nc.sync.dma_start(dst[:], src.rearrange("(p t) o -> p (t o)", t=PACK))
 
-        nc.scalar.dma_start(xt_all[:].bitcast(I32), xt_words[0].rearrange("p n t -> p (n t)").bitcast(I32))
+        nc.scalar.dma_start(w_raw[:].bitcast(I32), w_words[0].bitcast(I32))
         nc.sync.dma_start(ws_rows[:], w_scales[0].bitcast(I32).rearrange("(q r) c -> r q c", r=PACK))
         nc.sync.dma_start(l1[:], offs)
-        nc.sync.dma_start(w_raw[:].bitcast(I32), w_words[0].bitcast(I32))
         load_scale_rows(xs_all, xt_scales)
-        nc.sync.dma_start(l2[:], offs2)
+        nc.sync.dma_start(xt_all[:].bitcast(I32), xt_words[0].rearrange("p n t -> p (n t)").bitcast(I32))
         load_by_row(sg_sb, sg)
         load_by_row(bg_sb, bg)
-        nc.sync.dma_start(l4[:], offs4)
         load_by_row(sa_sb, sa)
+        nc.sync.dma_start(l4[:], offs4)
+        nc.sync.dma_start(l2[:], offs2)
         nc.sync.dma_start(l3[:], offs3)
         load_by_row(sb_sb, sb)
         nc.sync.dma_start(l5[:], offs5)
@@ -108,7 +108,7 @@ def tile_list_gatedladder_solo_one_pairweighed_kernel(
         ws_dst = ws_dealt[:].rearrange("p (t m) -> p t m", t=PACK)
         nc.vector.tensor_copy(ws_dst[:, 0, :], ws_src[:, 0, :])
         nc.vector.tensor_copy(xs_pick[:], xs_all[:].indirect(l1[:]))
-        xt_pick = keep.tile([P, J], U32, align_bytes=64, tag="xs_all_then_xt_pick")
+        xt_pick = keep.tile([P, J], U32, align_bytes=64)
         half = J // 2
         for s in range(2):
             nc.vector.tensor_copy(
@@ -139,12 +139,7 @@ def tile_list_gatedladder_solo_one_pairweighed_kernel(
             for i, t in enumerate(ts):
                 first_product(bank[:, i, :], t, slice(0, J))
             nc.scalar.copy(a_sb[:, ts[0] : ts[-1] + 1, :], bank[:])
-        for s in range(2):
-            nc.vector.tensor_copy(
-                pw[0][:].indirect(l2[:, half // 16 * s : half // 16 * (s + 1)]),
-                a_sb[:, 0, half * s : half * (s + 1)],
-            )
-        for t in range(1, PACK):
+        for t in range(PACK):
             nc.vector.tensor_copy(pw[t][:].indirect(l2[:]), a_sb[:, t, :])
 
         gate = [keep.tile([P, C], F32, name="gate0", align_bytes=64, tag="w_dealt_then_gate0")]

from contextlib import ExitStack

import concourse.mybir as mybir

K, T, J, R, C, O, N, U = 512, 1024, 256, 512, 512, 256, 256, 128
FLOPS = 2 * K * R * J + 2 * R * N * O

F32 = mybir.dt.float32
BF16 = mybir.dt.bfloat16
I32 = mybir.dt.int32
U32 = mybir.dt.uint32
U16 = mybir.dt.uint16
U8 = mybir.dt.uint8
E4M3X4 = mybir.dt.float8_e4m3fn_x4
E5M2X4 = mybir.dt.float8_e5m2_x4
E2M1X4 = mybir.dt.float4_e2m1fn_x4
ACT = mybir.ActivationFunctionType
ALU = mybir.AluOpType

P = 128
PACK = 4
QUADS = 4
QUAD = 32
BOARD = 2 * C


def tile_list_gatedladder_solo_one_pairweighed_kernel(
    tc, xt_words, xt_scales, w_words, w_scales, sa, sb, sg, bg, wb_words, wb_scales, so, sp,
    offs, offs2, offs3, offs4, offs5, offs6, offs7, out,
):
    nc = tc.nc
    with ExitStack() as ctx:
        keep = ctx.enter_context(tc.tile_pool(name="keep", bufs=1))
        psum = ctx.enter_context(tc.psum_pool(name="psum", bufs=1))

        def list_tile(name, src):
            return keep.tile(list(src.shape), U16, name=name)

        l1, l2, l3, l4 = list_tile("l1", offs), list_tile("l2", offs2), list_tile("l3", offs3), list_tile("l4", offs4)
        l5, l6, l7 = list_tile("l5", offs5), list_tile("l6", offs6), list_tile("l7", offs7)

        xt_all = keep.tile([P, T], U32, align_bytes=64)
        xs_all = keep.tile([P, T], U8, align_bytes=64)
        xs_pick = keep.tile([P, J], U8, align_bytes=64)
        w_raw = keep.tile([P, 2 * R], U8, align_bytes=64)
        w_dealt = keep.tile([P, 2 * R], U8, align_bytes=64, tag="w_dealt_then_gate0")
        ws_rows = keep.tile([PACK, QUADS, R // 4], I32, align_bytes=64)
        ws_raw = keep.tile([P, R], U8, align_bytes=64)
        ws_dealt = keep.tile([P, R], U8, align_bytes=64)
        wb_sb = keep.tile([P, N], U32, align_bytes=64)
        wbs_sb = keep.tile([P, N], U8, align_bytes=64)
        sa_sb = keep.tile([P, PACK], F32)
        sb_sb = keep.tile([P, PACK], F32)
        sg_sb = keep.tile([P, PACK], F32)
        bg_sb = keep.tile([P, PACK], F32)
        so_sb = keep.tile([P, N // P], F32)
        sp_sb = keep.tile([P, N // P], F32)
        pw = [keep.tile([P, BOARD], F32, name="pw%d" % t) for t in range(PACK)]

        nc.vector.memset(xs_all[:].bitcast(I32), 0)
        warm_in = keep.tile([P, 1], F32)
        warm_out = keep.tile([P, 1], F32)
        nc.vector.memset(warm_in[:], 0.0)
        nc.scalar.activation(warm_out[:], warm_in[:], ACT.Sigmoid)
        nc.vector.memset(ws_raw[:].bitcast(I32), 0)
        for t in range(PACK):
            nc.vector.memset(pw[t][:, 0:C], 0.0)
        nc.vector.memset(wbs_sb[:].bitcast(I32), 0)

        def load_scale_rows(plane, rows):
            for q in range(QUADS):
                nc.sync.dma_start(
                    plane[QUAD * q : QUAD * q + PACK, :].bitcast(I32),
                    rows[0, PACK * q : PACK * (q + 1), :].bitcast(I32),
                )

        def load_by_row(dst, src):
            nc.sync.dma_start(dst[:], src.rearrange("(p t) o -> p (t o)", t=PACK))

        nc.scalar.dma_start(w_raw[:].bitcast(I32), w_words[0].bitcast(I32))
        nc.sync.dma_start(ws_rows[:], w_scales[0].bitcast(I32).rearrange("(q r) c -> r q c", r=PACK))
        nc.sync.dma_start(l1[:], offs)
        load_scale_rows(xs_all, xt_scales)
        nc.sync.dma_start(xt_all[:].bitcast(I32), xt_words[0].rearrange("p n t -> p (n t)").bitcast(I32))
        load_by_row(sg_sb, sg)
        load_by_row(bg_sb, bg)
        load_by_row(sa_sb, sa)
        nc.sync.dma_start(l4[:], offs4)
        nc.sync.dma_start(l2[:], offs2)
        nc.sync.dma_start(l3[:], offs3)
        load_by_row(sb_sb, sb)
        nc.sync.dma_start(l5[:], offs5)
        nc.sync.dma_start(wb_sb[:].bitcast(I32), wb_words[0].rearrange("p n t -> p (n t)").bitcast(I32))
        load_scale_rows(wbs_sb, wb_scales)
        with nc.allow_non_contiguous_dma(reason="one weight a partition"):
            nc.sync.dma_start(so_sb[:], so.rearrange("(h p) o -> p (h o)", p=P))
            nc.sync.dma_start(sp_sb[:], sp.rearrange("(h p) o -> p (h o)", p=P))
        nc.sync.dma_start(l6[:], offs6)
        nc.sync.dma_start(l7[:], offs7)

        nc.scalar.copy(
            w_dealt[:].bitcast(U16).rearrange("p (t m) -> p t m", t=PACK),
            w_raw[:].bitcast(U16).rearrange("p (m t) -> p t m", t=PACK),
        )
        for q in range(QUADS):
            nc.vector.tensor_copy(ws_raw[QUAD * q : QUAD * q + PACK, :].bitcast(I32), ws_rows[:, q, :])
        ws_src = ws_raw[:].rearrange("p (m t) -> p t m", t=PACK)
        ws_dst = ws_dealt[:].rearrange("p (t m) -> p t m", t=PACK)
        nc.vector.tensor_copy(ws_dst[:, 0, :], ws_src[:, 0, :])
        nc.vector.tensor_copy(xs_pick[:], xs_all[:].indirect(l1[:]))
        xt_pick = keep.tile([P, J], U32, align_bytes=64)
        half = J // 2
        for s in range(2):
            nc.vector.tensor_copy(
                xt_pick[:, half * s : half * (s + 1)],
                xt_all[:].indirect(l1[:, half // 16 * s : half // 16 * (s + 1)]),
            )
        nc.vector.tensor_copy(ws_dst[:, 1:PACK, :], ws_src[:, 1:PACK, :])

        def first_product(bank, t, cols):
            nc.tensor.matmul_mx(
                bank,
                lhsT=w_dealt[:, 2 * P * t : 2 * P * (t + 1)].bitcast(E2M1X4),
                lhsT_scale=ws_dealt[:, P * t : P * (t + 1)],
                rhs=xt_pick[:, cols].bitcast(E4M3X4),
                rhs_scale=xs_pick[:, cols],
                start=True,
                stop=True,
            )

        a_sb = keep.tile([P, PACK, J], F32)
        for s in range(2):
            cols = slice(half * s, half * (s + 1))
            bank = psum.tile([P, half], F32, name="a_half%d" % s)
            first_product(bank[:], 0, cols)
            nc.scalar.copy(a_sb[:, 0, cols], bank[:])
        for ts in ((1,), (2, 3)):
            bank = psum.tile([P, len(ts), J], F32, name="a_bank%d" % ts[0])
            for i, t in enumerate(ts):
                first_product(bank[:, i, :], t, slice(0, J))
            nc.scalar.copy(a_sb[:, ts[0] : ts[-1] + 1, :], bank[:])
        for t in range(PACK):
            nc.vector.tensor_copy(pw[t][:].indirect(l2[:]), a_sb[:, t, :])

        gate = [keep.tile([P, C], F32, name="gate0", align_bytes=64, tag="w_dealt_then_gate0")]
        gate.extend(keep.tile([P, C], F32, name="gate%d" % t) for t in range(1, PACK))
        term = [keep.tile([P, C], F32, name="term%d" % t) for t in range(PACK)]
        for t in range(PACK):
            nc.scalar.activation(
                gate[t][:], pw[t][:].indirect(l4[:]), ACT.Sigmoid,
                bias=bg_sb[:, t : t + 1], scale=sg_sb[:, t : t + 1],
            )
            nc.scalar.activation(term[t][:], pw[t][:].indirect(l3[:]), ACT.Copy, scale=sa_sb[:, t : t + 1])

        gated = [keep.tile([P, C], F32, name="gated%d" % t) for t in range(PACK)]
        pg = [keep.tile([P, C], F32, name="pg%d" % t) for t in range(PACK)]
        for t in range(PACK):
            nc.vector.tensor_tensor(gated[t][:], term[t][:], gate[t][:], ALU.mult)
            nc.vector.tensor_tensor(pg[t][:], gated[t][:], pw[t][:, 0:C], ALU.max)

        hid = keep.tile([P, PACK, O], F32)
        for t in range(PACK - 1):
            nc.scalar.activation(hid[:, t, :], pg[t][:].indirect(l5[:]), ACT.Copy, scale=sb_sb[:, t : t + 1])
        part = O // 2
        t = PACK - 1
        for s in range(2):
            nc.scalar.activation(
                hid[:, t, part * s : part * (s + 1)],
                pg[t][:].indirect(l5[:, part // 16 * s : part // 16 * (s + 1)]),
                ACT.Copy, scale=sb_sb[:, t : t + 1],
            )

        hid_bf = keep.tile([P, O, PACK], BF16, align_bytes=64)
        hq = keep.tile([P, O], U32, align_bytes=64)
        hs = keep.tile([P, O], U8, align_bytes=64)
        nc.vector.tensor_copy(hid_bf[:, :, 0:2], hid[:, 0:2, :].rearrange("p t o -> p o t"))
        for s in range(2):
            cols = slice(part * s, part * (s + 1))
            nc.vector.tensor_copy(hid_bf[:, cols, 2:4], hid[:, 2:4, cols].rearrange("p t o -> p o t"))
        for s in range(2):
            cols = slice(part * s, part * (s + 1))
            nc.vector.quantize_mx(
                hq[:, cols].bitcast(E4M3X4), hs[:, cols], hid_bf[:, cols, :].rearrange("p o t -> p (o t)")
            )

        p_sb = [keep.tile([P, O], F32, name="p_sb%d" % h) for h in range(N // P)]
        for s in range(2):
            cols = slice(part * s, part * (s + 1))
            for h in range(N // P):
                p_bank = psum.tile([P, part], F32, name="p_bank%d_%d" % (s, h))
                nc.tensor.matmul_mx(
                    p_bank[:],
                    lhsT=wb_sb[:, P * h : P * (h + 1)].bitcast(E5M2X4),
                    lhsT_scale=wbs_sb[:, P * h : P * (h + 1)],
                    rhs=hq[:, cols].bitcast(E4M3X4),
                    rhs_scale=hs[:, cols],
                    start=True,
                    stop=True,
                )
                if h == 0:
                    nc.scalar.copy(p_sb[h][:, cols], p_bank[:])
                else:
                    nc.vector.tensor_copy(p_sb[h][:, cols], p_bank[:])
        for h in range(N // P):
            first = keep.tile([P, U], F32, name="first%d" % h)
            second = keep.tile([P, U], F32, name="second%d" % h)
            y = keep.tile([P, U], F32, name="y%d" % h)
            nc.scalar.activation(first[:], p_sb[h][:].indirect(l6[:]), ACT.Copy, scale=so_sb[:, h : h + 1])
            nc.scalar.activation(second[:], p_sb[h][:].indirect(l7[:]), ACT.Copy, scale=sp_sb[:, h : h + 1])
            nc.vector.tensor_tensor(y[:], first[:], second[:], ALU.max)
            nc.sync.dma_start(out[P * h : P * (h + 1), :], y[:])
